import numpy as np
import ml_dtypes


def mxq(x, axis, fmt="e4m3"):
    dtype, down = {"e4m3": (ml_dtypes.float8_e4m3fn, 7), "e5m2": (ml_dtypes.float8_e5m2, 14)}[fmt]
    v = np.moveaxis(np.asarray(x, np.float32).astype(ml_dtypes.bfloat16).astype(np.float64), axis, -1)
    blocks = v.reshape(v.shape[:-1] + (-1, 32))
    amax = np.abs(blocks).max(-1, keepdims=True)
    byte = np.maximum(np.where(amax > 0, np.frexp(amax)[1] - 1 + 127, 0) - down, 1)
    scale = np.exp2(byte - 127.0)
    codes = (blocks / scale).astype(np.float32).astype(dtype).astype(np.float64)
    return np.moveaxis((codes * scale).reshape(v.shape), -1, axis)


WIDE = False


def mx_kscale(k):
    if not WIDE:
        return np.ones(k)
    levels = np.array([10, -10, 5, -5, 0])
    if k % 512:
        return np.exp2(np.random.permutation(np.resize(levels, k // 32))).repeat(32)
    a = np.empty((k // 512, 16))
    for p in range(k // 512):
        a[p, :8] = np.random.permutation(np.resize(levels, 8))
        for g in range(8):
            far = levels[np.abs(levels - a[p, g]) >= 10]
            a[p, g + 8] = far[np.random.randint(len(far))]
    return np.exp2(a.ravel()).repeat(32)


def f64(x):
    return np.asarray(x).astype(np.float64)


def striped(idx):
    return np.tile(np.asarray(idx).reshape(-1, 16).T, (8, 1)).astype(np.uint16)


def unstriped(offs):
    return offs[:16].T.reshape(-1).astype(np.int64)


E2M1 = np.array([0.0, 0.5, 1.0, 1.5, 2.0, 3.0, 4.0, 6.0, -0.0, -0.5, -1.0, -1.5, -2.0, -3.0, -4.0, -6.0])


def pack_weight(w, fmt):
    k, n = w.shape
    w = f64(np.asarray(w, np.float32).astype(ml_dtypes.bfloat16)).reshape(k // 32, 32, n)
    amax = np.abs(w).max(1)
    if fmt == "e4m3":
        byte = np.frexp(amax)[1] - 1 + 127 - 7
    else:
        mant, ex = np.frexp(amax / 6.0)
        byte = np.where(mant > 0.5, ex, ex - 1) + 127
    byte = np.clip(np.where(amax > 0, byte, 1), 1, 254)
    scaled = (w * np.exp2(127.0 - byte)[:, None, :]).reshape(k, n).astype(np.float32)
    by_word = np.ascontiguousarray(scaled.reshape(k // 512, 128, 4, n).transpose(0, 1, 3, 2))
    if fmt == "e4m3":
        words = by_word.astype(ml_dtypes.float8_e4m3fn).view(np.uint8)
    else:
        c = by_word.astype(ml_dtypes.float4_e2m1fn).view(np.uint8) & 0xF
        words = (c[..., 0::2] | (c[..., 1::2] << 4)).reshape(k // 512, 128, 2 * n)
    return np.ascontiguousarray(words), np.ascontiguousarray(byte.astype(np.uint8).reshape(k // 512, 16, n))


def unpack_weight(words, scales, fmt):
    g, _, n = scales.shape
    words = np.ascontiguousarray(words).reshape(g, 128, n, -1)
    if fmt == "e4m3":
        vals = words.view(ml_dtypes.float8_e4m3fn).astype(np.float64)
    else:
        nib = np.empty((g, 128, n, 4), np.uint8)
        nib[..., 0::2] = words & 0xF
        nib[..., 1::2] = words >> 4
        vals = E2M1[nib]
    vals = vals * np.repeat(np.exp2(scales.astype(np.float64) - 127.0), 8, axis=1)[..., None]
    return vals.transpose(0, 1, 3, 2).reshape(g * 512, n)


def sigmoid(v):
    return 1.0 / (1.0 + np.exp(-v))


K, T, J, N = 1024, 1024, 512, 512


def setup_inputs():
    n = np.random.standard_normal
    idx = np.random.permutation(T)[:J]
    idx2 = np.random.permutation(T)[:J]
    fk = mx_kscale(K)
    wap = pack_weight(n((K, N)) * 1 / np.sqrt(K) * fk[:, None], "e2m1")
    wbp = pack_weight(n((K, N)) * 1 / np.sqrt(K) * fk[:, None], "e4m3")
    return {
        "xq": (n((K, T)) / fk[:, None]).astype(np.float32),
        "wa_words": wap[0],
        "wa_scales": wap[1],
        "wb_words": wbp[0],
        "wb_scales": wbp[1],
        "gate": (1.0 * n((N, T))).astype(np.float32),
        "offs": striped(idx),
        "offs2": striped(idx2),
    }


def reference(xq, wa_words, wa_scales, wb_words, wb_scales, gate, offs, offs2):
    idx = unstriped(offs)
    idx2 = unstriped(offs2)
    wau = unpack_weight(wa_words, wa_scales, "e2m1")
    wbu = unpack_weight(wb_words, wb_scales, "e4m3")
    xqidxq = mxq(f64(xq)[:, idx], 0, "e4m3")
    p = wau.T @ xqidxq
    xqidx2q = mxq(f64(xq)[:, idx2], 0, "e4m3")
    q = wbu.T @ xqidx2q
    pg = np.zeros((N, T))
    pg[:, idx2] = p
    qg = np.zeros((N, T))
    qg[:, idx] = q
    y = (pg + qg) * sigmoid(f64(gate))
    return y

@@ -1,0 +1,158 @@
+from contextlib import ExitStack
+
+import concourse.mybir as mybir
+
+K, T, J, N = 1024, 1024, 512, 512
+FLOPS = 2 * 2 * K * J * N
+
+F32 = mybir.dt.float32
+BF16 = mybir.dt.bfloat16
+I32 = mybir.dt.int32
+U32 = mybir.dt.uint32
+U16 = mybir.dt.uint16
+U8 = mybir.dt.uint8
+FP8X4 = mybir.dt.float8_e4m3fn_x4
+FP4X4 = mybir.dt.float4_e2m1fn_x4
+ACT = mybir.ActivationFunctionType
+ALU = mybir.AluOpType
+
+P = 128
+PASSES = K // 512
+TILES = N // P
+HALF = T // 2
+
+
+def tile_list_experts_exchange_kernel(tc, xq, wa_words, wa_scales, wb_words, wb_scales, gate, offs, offs2, out):
+    nc = tc.nc
+    with ExitStack() as ctx:
+        keep = ctx.enter_context(tc.tile_pool(name="keep", bufs=1))
+        psum = ctx.enter_context(tc.psum_pool(name="psum", bufs=1))
+
+        lists = [keep.tile([P, J // 16], U16, name=f"list{e}") for e in range(2)]
+        nc.sync.dma_start(lists[0][:], offs)
+        nc.sync.dma_start(lists[1][:], offs2)
+
+        w_scales = [keep.tile([P, PASSES, N], U8, name=f"w_scales{e}", align_bytes=64) for e in range(2)]
+        for e in range(2):
+            nc.vector.memset(w_scales[e][:].rearrange("p a n -> p (a n)").bitcast(I32), 0)
+
+        x_rows = xq.rearrange("(a p u e) t -> a u p e t", a=PASSES, p=P, u=2, e=2)
+        raw = {}
+        for a in range(PASSES):
+            for u in range(2):
+                for h in range(2):
+                    raw[a, u, h] = keep.tile([P, 2, HALF], F32, name=f"raw{a}{u}{h}")
+                    nc.sync.dma_start(raw[a, u, h][:], x_rows[a, u][:, :, h * HALF:(h + 1) * HALF])
+
+        wa = keep.tile([P, PASSES, 2 * N], U8, name="wa", align_bytes=64)
+        wb = keep.tile([P, PASSES, 4 * N], U8, name="wb", align_bytes=64)
+        for e, (tile, words, scales) in enumerate((
+            (wa, wa_words, wa_scales),
+            (wb, wb_words.rearrange("a p n r -> a p (n r)"), wb_scales),
+        )):
+            for q in range(4):
+                nc.sync.dma_start(
+                    w_scales[e][32 * q:32 * q + 4].bitcast(I32),
+                    scales[:, 4 * q:4 * q + 4, :].rearrange("a r n -> r a n").bitcast(I32),
+                )
+            nc.sync.dma_start(tile[:].bitcast(I32), words.rearrange("a p c -> p a c").bitcast(I32))
+
+        gates = [keep.tile([P, T], F32, name=f"gate{i}") for i in range(TILES)]
+        for i in range(TILES):
+            nc.sync.dma_start(gates[i][:], gate[i * P:(i + 1) * P, :])
+
+        pages = {}
+        for i in range(TILES):
+            for e in range(2):
+                pages[e, i] = keep.tile([P, T], F32, name=f"page{e}{i}")
+                nc.vector.memset(pages[e, i][:].bitcast(I32), 0)
+
+        pairs, picked, woven, codes, planes = {}, {}, {}, {}, {}
+        for a in range(PASSES):
+            for u in range(2):
+                pairs[a, u] = keep.tile([P, T], F32, name=f"pairs{a}{u}")
+            for e in range(2):
+                picked[e, a] = keep.tile([P, 2, J], F32, name=f"picked{e}{a}")
+                woven[e, a] = keep.tile([P, 2 * J], F32, name=f"woven{e}{a}", align_bytes=64)
+                codes[e, a] = keep.tile([P, J], U32, name=f"codes{e}{a}", align_bytes=64)
+                planes[e, a] = keep.tile([P, J], U8, name=f"plane{e}{a}", align_bytes=64)
+        first_bank = psum.tile([P, J], F32, name="first_bank")
+        later_bank = psum.tile([P, J], F32, name="later_bank")
+        banks = {(e, i): later_bank if e + i else first_bank for e in range(2) for i in range(TILES)}
+        sums = {(e, i): keep.tile([P, J], F32, name=f"sum{e}{i}") for e in range(2) for i in range(TILES)}
+        sig = [keep.tile([P, T], F32, name=f"sig{i}") for i in range(TILES)]
+        both = [keep.tile([P, T], F32, name=f"both{i}") for i in range(TILES)]
+
+        def cast(a, u):
+            for h in range(2):
+                dst = pairs[a, u][:, h * HALF:(h + 1) * HALF].bitcast(BF16).rearrange("p (t e) -> p t e", e=2)
+                src = raw[a, u, h][:].rearrange("p e t -> p t e")
+                if (a, u, h) == (0, 0, 1):
+                    nc.vector.tensor_copy(dst, src)
+                else:
+                    nc.scalar.activation(dst, src, ACT.Copy)
+
+        def pick(e, a, u):
+            nc.vector.tensor_copy(picked[e, a][:, u, :], pairs[a, u][:].indirect(lists[e][:]))
+
+        def weave(e, a):
+            nc.scalar.copy(woven[e, a][:].rearrange("p (j u) -> p j u", u=2), picked[e, a][:].rearrange("p u j -> p j u"))
+
+        def quantize(e, a):
+            nc.vector.quantize_mx(out=codes[e, a][:].bitcast(FP8X4), scales=planes[e, a][:], in_=woven[e, a][:].bitcast(BF16))
+
+        def multiply(e, a, i):
+            if e == 0:
+                lhsT = wa[:, a, 2 * P * i:2 * P * (i + 1)].bitcast(FP4X4)
+            else:
+                lhsT = wb[:, a, 4 * P * i:4 * P * (i + 1)].bitcast(FP8X4)
+            nc.tensor.matmul_mx(
+                out=banks[e, i][:], lhsT=lhsT, lhsT_scale=w_scales[e][:, a, P * i:P * (i + 1)],
+                rhs=codes[e, a][:].bitcast(FP8X4), rhs_scale=planes[e, a][:],
+                start=(a == 0), stop=(a == PASSES - 1),
+            )
+
+        cast(0, 0)
+        pick(0, 0, 0)
+        pick(1, 0, 0)
+        cast(0, 1)
+        pick(0, 0, 1)
+        pick(1, 0, 1)
+        cast(1, 0)
+        weave(0, 0)
+        pick(0, 1, 0)
+        pick(1, 1, 0)
+        quantize(0, 0)
+        cast(1, 1)
+        multiply(0, 0, 0)
+        pick(0, 1, 1)
+        weave(0, 1)
+        pick(1, 1, 1)
+        quantize(0, 1)
+        multiply(0, 1, 0)
+        nc.scalar.copy(sums[0, 0][:], banks[0, 0][:])
+        for a in range(PASSES):
+            weave(1, a)
+            quantize(1, a)
+
+        for i in range(TILES):
+            for e in range(2):
+                if e + i:
+                    for a in range(PASSES):
+                        multiply(e, a, i)
+                    nc.scalar.copy(sums[e, i][:], banks[e, i][:])
+            nc.scalar.activation(sig[i][:], gates[i][:], ACT.Sigmoid)
+            nc.vector.tensor_copy(pages[0, i][:].indirect(lists[1][:]), sums[0, i][:])
+            nc.vector.tensor_copy(pages[1, i][:].indirect(lists[0][:]), sums[1, i][:])
+            rows = slice(i * P, (i + 1) * P)
+            if i < TILES - 1:
+                nc.gpsimd.tensor_tensor(both[i][:], pages[0, i][:], pages[1, i][:], ALU.add)
+                nc.gpsimd.tensor_tensor(gates[i][:], both[i][:], sig[i][:], ALU.mult)
+                nc.sync.dma_start(out[rows, :], gates[i][:])
+            else:
+                halves = [slice(h * HALF, (h + 1) * HALF) for h in range(2)]
+                for cols in halves:
+                    nc.vector.tensor_tensor(both[i][:, cols], pages[0, i][:, cols], pages[1, i][:, cols], ALU.add)
+                for cols in halves:
+                    nc.vector.tensor_tensor(gates[i][:, cols], both[i][:, cols], sig[i][:, cols], ALU.mult)
+                    nc.sync.dma_start(out[rows, cols], gates[i][:, cols])

@@ -20,6 +20,7 @@ P = 128
 PASSES = K // 512
 TILES = N // P
 HALF = T // 2
+LAST_CUTS = (0, 512, 896, 1024)
 
 
 def tile_list_experts_exchange_kernel(tc, xq, wa_words, wa_scales, wb_words, wb_scales, gate, offs, offs2, out):
@@ -28,21 +29,35 @@ def tile_list_experts_exchange_kernel(tc, xq, wa_words, wa_scales, wb_words, wb_
         keep = ctx.enter_context(tc.tile_pool(name="keep", bufs=1))
         psum = ctx.enter_context(tc.psum_pool(name="psum", bufs=1))
 
-        lists = [keep.tile([P, J // 16], U16, name=f"list{e}") for e in range(2)]
-        nc.sync.dma_start(lists[0][:], offs)
-        nc.sync.dma_start(lists[1][:], offs2)
-
         w_scales = [keep.tile([P, PASSES, N], U8, name=f"w_scales{e}", align_bytes=64) for e in range(2)]
         for e in range(2):
             nc.vector.memset(w_scales[e][:].rearrange("p a n -> p (a n)").bitcast(I32), 0)
+        pages = {}
+        for s in range(2):
+            for e in range(2):
+                pages[e, s] = keep.tile([P, T], F32, name=f"page{e}{s}")
+                (nc.gpsimd if s else nc.vector).memset(pages[e, s][:].bitcast(I32), 0)
 
         x_rows = xq.rearrange("(a p u e) t -> a u p e t", a=PASSES, p=P, u=2, e=2)
         raw = {}
-        for a in range(PASSES):
-            for u in range(2):
-                for h in range(2):
-                    raw[a, u, h] = keep.tile([P, 2, HALF], F32, name=f"raw{a}{u}{h}")
-                    nc.sync.dma_start(raw[a, u, h][:], x_rows[a, u][:, :, h * HALF:(h + 1) * HALF])
+
+        def load_pair(a, u):
+            for h in range(2):
+                raw[a, u, h] = keep.tile([P, 2, HALF], F32, name=f"raw{a}{u}{h}", align_bytes=64)
+                nc.sync.dma_start(raw[a, u, h][:], x_rows[a, u][:, :, h * HALF:(h + 1) * HALF])
+
+        load_pair(0, 0)
+        lists = [keep.tile([P, J // 16], U16, name=f"list{e}") for e in range(2)]
+        nc.sync.dma_start(lists[0][:], offs)
+        nc.sync.dma_start(lists[1][:], offs2)
+        end_cols = slice(LAST_CUTS[-2], T)
+        end_gate = keep.tile([P, T - LAST_CUTS[-2]], F32, name="end_gate")
+        end_sig = keep.tile([P, T - LAST_CUTS[-2]], F32, name="end_sig")
+        nc.sync.dma_start(end_gate[:], gate[N - P:N, end_cols])
+        nc.scalar.activation(end_sig[:], end_gate[:], ACT.Sigmoid)
+        load_pair(0, 1)
+        load_pair(1, 0)
+        load_pair(1, 1)
 
         wa = keep.tile([P, PASSES, 2 * N], U8, name="wa", align_bytes=64)
         wb = keep.tile([P, PASSES, 4 * N], U8, name="wb", align_bytes=64)
@@ -50,53 +65,51 @@ def tile_list_experts_exchange_kernel(tc, xq, wa_words, wa_scales, wb_words, wb_
             (wa, wa_words, wa_scales),
             (wb, wb_words.rearrange("a p n r -> a p (n r)"), wb_scales),
         )):
+            nc.sync.dma_start(tile[:].bitcast(I32), words.rearrange("a p c -> p a c").bitcast(I32))
             for q in range(4):
                 nc.sync.dma_start(
                     w_scales[e][32 * q:32 * q + 4].bitcast(I32),
                     scales[:, 4 * q:4 * q + 4, :].rearrange("a r n -> r a n").bitcast(I32),
                 )
-            nc.sync.dma_start(tile[:].bitcast(I32), words.rearrange("a p c -> p a c").bitcast(I32))
 
+        widths = [T] * (TILES - 1) + [LAST_CUTS[-2]]
         gates = [keep.tile([P, T], F32, name=f"gate{i}") for i in range(TILES)]
         for i in range(TILES):
-            nc.sync.dma_start(gates[i][:], gate[i * P:(i + 1) * P, :])
-
-        pages = {}
-        for i in range(TILES):
-            for e in range(2):
-                pages[e, i] = keep.tile([P, T], F32, name=f"page{e}{i}")
-                nc.vector.memset(pages[e, i][:].bitcast(I32), 0)
+            nc.sync.dma_start(gates[i][:, :widths[i]], gate[i * P:(i + 1) * P, :widths[i]])
 
         pairs, picked, woven, codes, planes = {}, {}, {}, {}, {}
         for a in range(PASSES):
             for u in range(2):
-                pairs[a, u] = keep.tile([P, T], F32, name=f"pairs{a}{u}")
+                pairs[a, u] = keep.tile([P, T], F32, name=f"pairs{a}{u}", align_bytes=64)
             for e in range(2):
-                picked[e, a] = keep.tile([P, 2, J], F32, name=f"picked{e}{a}")
-                woven[e, a] = keep.tile([P, 2 * J], F32, name=f"woven{e}{a}", align_bytes=64)
+                picked[e, a] = keep.tile([P, 2 * J], F32, name=f"picked{e}{a}", align_bytes=64)
                 codes[e, a] = keep.tile([P, J], U32, name=f"codes{e}{a}", align_bytes=64)
                 planes[e, a] = keep.tile([P, J], U8, name=f"plane{e}{a}", align_bytes=64)
         first_bank = psum.tile([P, J], F32, name="first_bank")
         later_bank = psum.tile([P, J], F32, name="later_bank")
         banks = {(e, i): later_bank if e + i else first_bank for e in range(2) for i in range(TILES)}
         sums = {(e, i): keep.tile([P, J], F32, name=f"sum{e}{i}") for e in range(2) for i in range(TILES)}
-        sig = [keep.tile([P, T], F32, name=f"sig{i}") for i in range(TILES)]
         both = [keep.tile([P, T], F32, name=f"both{i}") for i in range(TILES)]
 
-        def cast(a, u):
-            for h in range(2):
-                dst = pairs[a, u][:, h * HALF:(h + 1) * HALF].bitcast(BF16).rearrange("p (t e) -> p t e", e=2)
-                src = raw[a, u, h][:].rearrange("p e t -> p t e")
-                if (a, u, h) == (0, 0, 1):
-                    nc.vector.tensor_copy(dst, src)
-                else:
-                    nc.scalar.activation(dst, src, ACT.Copy)
+        def cast(a, u, h, lo, hi, on_vector):
+            dst = pairs[a, u][:, h * HALF + lo:h * HALF + hi].bitcast(BF16).rearrange("p (t e) -> p t e", e=2)
+            src = raw[a, u, h][:, :, lo:hi].rearrange("p e t -> p t e")
+            if on_vector:
+                nc.vector.tensor_copy(dst, src)
+            else:
+                nc.scalar.activation(dst, src, ACT.Copy)
 
         def pick(e, a, u):
-            nc.vector.tensor_copy(picked[e, a][:, u, :], pairs[a, u][:].indirect(lists[e][:]))
+            nc.vector.tensor_copy(picked[e, a][:, u * J:(u + 1) * J], pairs[a, u][:].indirect(lists[e][:]))
 
-        def weave(e, a):
-            nc.scalar.copy(woven[e, a][:].rearrange("p (j u) -> p j u", u=2), picked[e, a][:].rearrange("p u j -> p j u"))
+        def weave(e, a, on_vector, tag):
+            woven[e, a] = keep.tile([P, 2 * J], F32, name=f"woven{e}{a}", tag=tag, align_bytes=64)
+            dst = woven[e, a][:].rearrange("p (j u) -> p j u", u=2)
+            src = picked[e, a][:].rearrange("p (u j) -> p j u", u=2)
+            if on_vector:
+                nc.vector.tensor_copy(dst, src)
+            else:
+                nc.scalar.copy(dst, src)
 
         def quantize(e, a):
             nc.vector.quantize_mx(out=codes[e, a][:].bitcast(FP8X4), scales=planes[e, a][:], in_=woven[e, a][:].bitcast(BF16))
@@ -112,28 +125,34 @@ def tile_list_experts_exchange_kernel(tc, xq, wa_words, wa_scales, wb_words, wb_
                 start=(a == 0), stop=(a == PASSES - 1),
             )
 
-        cast(0, 0)
+        cast(0, 0, 0, 0, HALF, True)
+        cast(0, 0, 1, 0, HALF, True)
         pick(0, 0, 0)
         pick(1, 0, 0)
-        cast(0, 1)
+        cast(0, 1, 0, 0, HALF, False)
+        cast(0, 1, 1, 0, HALF // 2, False)
+        cast(0, 1, 1, HALF // 2, HALF, True)
         pick(0, 0, 1)
         pick(1, 0, 1)
-        cast(1, 0)
-        weave(0, 0)
+        weave(0, 0, True, "woven00")
+        cast(1, 0, 0, 0, HALF, False)
+        cast(1, 0, 1, 0, HALF, False)
         pick(0, 1, 0)
-        pick(1, 1, 0)
         quantize(0, 0)
-        cast(1, 1)
+        pick(1, 1, 0)
+        cast(1, 1, 0, 0, HALF, False)
+        cast(1, 1, 1, 0, HALF, False)
         multiply(0, 0, 0)
         pick(0, 1, 1)
-        weave(0, 1)
+        weave(0, 1, False, "woven01")
         pick(1, 1, 1)
         quantize(0, 1)
         multiply(0, 1, 0)
+        weave(1, 0, False, "raw111")
+        quantize(1, 0)
         nc.scalar.copy(sums[0, 0][:], banks[0, 0][:])
-        for a in range(PASSES):
-            weave(1, a)
-            quantize(1, a)
+        weave(1, 1, False, "woven11")
+        quantize(1, 1)
 
         for i in range(TILES):
             for e in range(2):
@@ -141,18 +160,21 @@ def tile_list_experts_exchange_kernel(tc, xq, wa_words, wa_scales, wb_words, wb_
                     for a in range(PASSES):
                         multiply(e, a, i)
                     nc.scalar.copy(sums[e, i][:], banks[e, i][:])
-            nc.scalar.activation(sig[i][:], gates[i][:], ACT.Sigmoid)
-            nc.vector.tensor_copy(pages[0, i][:].indirect(lists[1][:]), sums[0, i][:])
-            nc.vector.tensor_copy(pages[1, i][:].indirect(lists[0][:]), sums[1, i][:])
+            sig = keep.tile([P, T], F32, name=f"sig{i}", tag=("picked11", "woven11")[i % 2], align_bytes=64)
+            nc.scalar.activation(sig[:, :widths[i]], gates[i][:, :widths[i]], ACT.Sigmoid)
+            page_p, page_q = pages[0, i % 2], pages[1, i % 2]
+            nc.vector.tensor_copy(page_p[:].indirect(lists[1][:]), sums[0, i][:])
+            nc.vector.tensor_copy(page_q[:].indirect(lists[0][:]), sums[1, i][:])
             rows = slice(i * P, (i + 1) * P)
             if i < TILES - 1:
-                nc.gpsimd.tensor_tensor(both[i][:], pages[0, i][:], pages[1, i][:], ALU.add)
-                nc.gpsimd.tensor_tensor(gates[i][:], both[i][:], sig[i][:], ALU.mult)
+                nc.gpsimd.tensor_tensor(both[i][:], page_p[:], page_q[:], ALU.add)
+                nc.gpsimd.tensor_tensor(gates[i][:], both[i][:], sig[:], ALU.mult)
                 nc.sync.dma_start(out[rows, :], gates[i][:])
             else:
-                halves = [slice(h * HALF, (h + 1) * HALF) for h in range(2)]
-                for cols in halves:
-                    nc.vector.tensor_tensor(both[i][:, cols], pages[0, i][:, cols], pages[1, i][:, cols], ALU.add)
-                for cols in halves:
-                    nc.vector.tensor_tensor(gates[i][:, cols], both[i][:, cols], sig[i][:, cols], ALU.mult)
+                cuts = [slice(lo, hi) for lo, hi in zip(LAST_CUTS, LAST_CUTS[1:])]
+                for cols in cuts:
+                    nc.vector.tensor_tensor(both[i][:, cols], page_p[:, cols], page_q[:, cols], ALU.add)
+                for cols in cuts:
+                    factor = end_sig[:] if cols == end_cols else sig[:, cols]
+                    nc.vector.tensor_tensor(gates[i][:, cols], both[i][:, cols], factor, ALU.mult)
                     nc.sync.dma_start(out[rows, cols], gates[i][:, cols])

@@ -21,6 +21,7 @@ PASSES = K // 512
 TILES = N // P
 HALF = T // 2
 LAST_CUTS = (0, 512, 896, 1024)
+EARLY = 64
 
 
 def tile_list_experts_exchange_kernel(tc, xq, wa_words, wa_scales, wb_words, wb_scales, gate, offs, offs2, out):
@@ -42,19 +43,19 @@ def tile_list_experts_exchange_kernel(tc, xq, wa_words, wa_scales, wb_words, wb_
         raw = {}
 
         def load_pair(a, u):
-            for h in range(2):
-                raw[a, u, h] = keep.tile([P, 2, HALF], F32, name=f"raw{a}{u}{h}", align_bytes=64)
-                nc.sync.dma_start(raw[a, u, h][:], x_rows[a, u][:, :, h * HALF:(h + 1) * HALF])
+            cuts = (0, 512, 1024)
+            for h, (lo, hi) in enumerate(zip(cuts, cuts[1:])):
+                raw[a, u, h] = (keep.tile([P, 2, hi - lo], F32, name=f"raw{a}{u}{h}", align_bytes=64), lo)
+                nc.sync.dma_start(raw[a, u, h][0][:], x_rows[a, u][:, :, lo:hi])
 
         load_pair(0, 0)
         lists = [keep.tile([P, J // 16], U16, name=f"list{e}") for e in range(2)]
         nc.sync.dma_start(lists[0][:], offs)
         nc.sync.dma_start(lists[1][:], offs2)
-        end_cols = slice(LAST_CUTS[-2], T)
-        end_gate = keep.tile([P, T - LAST_CUTS[-2]], F32, name="end_gate")
-        end_sig = keep.tile([P, T - LAST_CUTS[-2]], F32, name="end_sig")
-        nc.sync.dma_start(end_gate[:], gate[N - P:N, end_cols])
-        nc.scalar.activation(end_sig[:], end_gate[:], ACT.Sigmoid)
+        sigs = [keep.tile([P, T], F32, name=f"sig{i}") for i in range(TILES)]
+        early_gate = keep.tile([P, EARLY], F32, name="early_gate")
+        nc.sync.dma_start(early_gate[:], gate[N - P:N, T - EARLY:T])
+        nc.scalar.activation(sigs[-1][:, T - EARLY:T], early_gate[:], ACT.Sigmoid)
         load_pair(0, 1)
         load_pair(1, 0)
         load_pair(1, 1)
@@ -72,7 +73,7 @@ def tile_list_experts_exchange_kernel(tc, xq, wa_words, wa_scales, wb_words, wb_
                     scales[:, 4 * q:4 * q + 4, :].rearrange("a r n -> r a n").bitcast(I32),
                 )
 
-        widths = [T] * (TILES - 1) + [LAST_CUTS[-2]]
+        widths = [T] * (TILES - 1) + [T - EARLY]
         gates = [keep.tile([P, T], F32, name=f"gate{i}") for i in range(TILES)]
         for i in range(TILES):
             nc.sync.dma_start(gates[i][:, :widths[i]], gate[i * P:(i + 1) * P, :widths[i]])
@@ -92,8 +93,9 @@ def tile_list_experts_exchange_kernel(tc, xq, wa_words, wa_scales, wb_words, wb_
         both = [keep.tile([P, T], F32, name=f"both{i}") for i in range(TILES)]
 
         def cast(a, u, h, lo, hi, on_vector):
-            dst = pairs[a, u][:, h * HALF + lo:h * HALF + hi].bitcast(BF16).rearrange("p (t e) -> p t e", e=2)
-            src = raw[a, u, h][:, :, lo:hi].rearrange("p e t -> p t e")
+            tile, base = raw[a, u, h]
+            dst = pairs[a, u][:, base + lo:base + hi].bitcast(BF16).rearrange("p (t e) -> p t e", e=2)
+            src = tile[:, :, lo:hi].rearrange("p e t -> p t e")
             if on_vector:
                 nc.vector.tensor_copy(dst, src)
             else:
@@ -127,32 +129,26 @@ def tile_list_experts_exchange_kernel(tc, xq, wa_words, wa_scales, wb_words, wb_
 
         cast(0, 0, 0, 0, HALF, True)
         cast(0, 0, 1, 0, HALF, True)
-        pick(0, 0, 0)
-        pick(1, 0, 0)
-        cast(0, 1, 0, 0, HALF, False)
-        cast(0, 1, 1, 0, HALF // 2, False)
-        cast(0, 1, 1, HALF // 2, HALF, True)
-        pick(0, 0, 1)
-        pick(1, 0, 1)
-        weave(0, 0, True, "woven00")
-        cast(1, 0, 0, 0, HALF, False)
-        cast(1, 0, 1, 0, HALF, False)
-        pick(0, 1, 0)
-        quantize(0, 0)
-        pick(1, 1, 0)
-        cast(1, 1, 0, 0, HALF, False)
-        cast(1, 1, 1, 0, HALF, False)
-        multiply(0, 0, 0)
-        pick(0, 1, 1)
+        for a, u in ((0, 0), (0, 1), (1, 0), (1, 1)):
+            if a + u:
+                cast(a, u, 0, 0, HALF, False)
+                if (a, u) == (0, 1):
+                    cast(a, u, 1, 0, 256, False)
+                    cast(a, u, 1, 256, HALF, True)
+                else:
+                    cast(a, u, 1, 0, HALF, False)
+            pick(0, a, u)
+            pick(1, a, u)
+        weave(0, 0, False, "raw111")
+        weave(1, 0, False, "picked00")
         weave(0, 1, False, "woven01")
-        pick(1, 1, 1)
-        quantize(0, 1)
-        multiply(0, 1, 0)
-        weave(1, 0, False, "raw111")
-        quantize(1, 0)
-        nc.scalar.copy(sums[0, 0][:], banks[0, 0][:])
         weave(1, 1, False, "woven11")
-        quantize(1, 1)
+        for e in range(2):
+            for a in range(PASSES):
+                quantize(e, a)
+        for a in range(PASSES):
+            multiply(0, a, 0)
+        nc.scalar.copy(sums[0, 0][:], banks[0, 0][:])
 
         for i in range(TILES):
             for e in range(2):
@@ -160,7 +156,7 @@ def tile_list_experts_exchange_kernel(tc, xq, wa_words, wa_scales, wb_words, wb_
                     for a in range(PASSES):
                         multiply(e, a, i)
                     nc.scalar.copy(sums[e, i][:], banks[e, i][:])
-            sig = keep.tile([P, T], F32, name=f"sig{i}", tag=("picked11", "woven11")[i % 2], align_bytes=64)
+            sig = sigs[i]
             nc.scalar.activation(sig[:, :widths[i]], gates[i][:, :widths[i]], ACT.Sigmoid)
             page_p, page_q = pages[0, i % 2], pages[1, i % 2]
             nc.vector.tensor_copy(page_p[:].indirect(lists[1][:]), sums[0, i][:])
@@ -175,6 +171,5 @@ def tile_list_experts_exchange_kernel(tc, xq, wa_words, wa_scales, wb_words, wb_
                 for cols in cuts:
                     nc.vector.tensor_tensor(both[i][:, cols], page_p[:, cols], page_q[:, cols], ALU.add)
                 for cols in cuts:
-                    factor = end_sig[:] if cols == end_cols else sig[:, cols]
-                    nc.vector.tensor_tensor(gates[i][:, cols], both[i][:, cols], factor, ALU.mult)
+                    nc.vector.tensor_tensor(gates[i][:, cols], both[i][:, cols], sig[:, cols], ALU.mult)
                     nc.sync.dma_start(out[rows, cols], gates[i][:, cols])

from contextlib import ExitStack

import concourse.mybir as mybir

K, T, J, N = 1024, 1024, 512, 512
FLOPS = 2 * 2 * K * J * N

F32 = mybir.dt.float32
BF16 = mybir.dt.bfloat16
I32 = mybir.dt.int32
U32 = mybir.dt.uint32
U16 = mybir.dt.uint16
U8 = mybir.dt.uint8
FP8X4 = mybir.dt.float8_e4m3fn_x4
FP4X4 = mybir.dt.float4_e2m1fn_x4
ACT = mybir.ActivationFunctionType
ALU = mybir.AluOpType

P = 128
PASSES = K // 512
TILES = N // P
HALF = T // 2
LAST_CUTS = (0, 512, 896, 1024)
EARLY = 64


def tile_list_experts_exchange_kernel(tc, xq, wa_words, wa_scales, wb_words, wb_scales, gate, offs, offs2, out):
    nc = tc.nc
    with ExitStack() as ctx:
        keep = ctx.enter_context(tc.tile_pool(name="keep", bufs=1))
        psum = ctx.enter_context(tc.psum_pool(name="psum", bufs=1))

        w_scales = [keep.tile([P, PASSES, N], U8, name=f"w_scales{e}", align_bytes=64) for e in range(2)]
        for e in range(2):
            nc.vector.memset(w_scales[e][:].rearrange("p a n -> p (a n)").bitcast(I32), 0)
        pages = {}
        for s in range(2):
            for e in range(2):
                pages[e, s] = keep.tile([P, T], F32, name=f"page{e}{s}")
                (nc.gpsimd if s else nc.vector).memset(pages[e, s][:].bitcast(I32), 0)

        x_rows = xq.rearrange("(a p u e) t -> a u p e t", a=PASSES, p=P, u=2, e=2)
        raw = {}

        def load_pair(a, u):
            cuts = (0, 512, 1024)
            for h, (lo, hi) in enumerate(zip(cuts, cuts[1:])):
                raw[a, u, h] = (keep.tile([P, 2, hi - lo], F32, name=f"raw{a}{u}{h}", align_bytes=64), lo)
                nc.sync.dma_start(raw[a, u, h][0][:], x_rows[a, u][:, :, lo:hi])

        load_pair(0, 0)
        lists = [keep.tile([P, J // 16], U16, name=f"list{e}") for e in range(2)]
        nc.sync.dma_start(lists[0][:], offs)
        nc.sync.dma_start(lists[1][:], offs2)
        sigs = [keep.tile([P, T], F32, name=f"sig{i}") for i in range(TILES)]
        early_gate = keep.tile([P, EARLY], F32, name="early_gate")
        nc.sync.dma_start(early_gate[:], gate[N - P:N, T - EARLY:T])
        nc.scalar.activation(sigs[-1][:, T - EARLY:T], early_gate[:], ACT.Sigmoid)
        load_pair(0, 1)
        load_pair(1, 0)
        load_pair(1, 1)

        wa = keep.tile([P, PASSES, 2 * N], U8, name="wa", align_bytes=64)
        wb = keep.tile([P, PASSES, 4 * N], U8, name="wb", align_bytes=64)
        for e, (tile, words, scales) in enumerate((
            (wa, wa_words, wa_scales),
            (wb, wb_words.rearrange("a p n r -> a p (n r)"), wb_scales),
        )):
            nc.sync.dma_start(tile[:].bitcast(I32), words.rearrange("a p c -> p a c").bitcast(I32))
            for q in range(4):
                nc.sync.dma_start(
                    w_scales[e][32 * q:32 * q + 4].bitcast(I32),
                    scales[:, 4 * q:4 * q + 4, :].rearrange("a r n -> r a n").bitcast(I32),
                )

        widths = [T] * (TILES - 1) + [T - EARLY]
        gates = [keep.tile([P, T], F32, name=f"gate{i}") for i in range(TILES)]
        for i in range(TILES):
            nc.sync.dma_start(gates[i][:, :widths[i]], gate[i * P:(i + 1) * P, :widths[i]])

        pairs, picked, woven, codes, planes = {}, {}, {}, {}, {}
        for a in range(PASSES):
            for u in range(2):
                pairs[a, u] = keep.tile([P, T], F32, name=f"pairs{a}{u}", align_bytes=64)
            for e in range(2):
                picked[e, a] = keep.tile([P, 2 * J], F32, name=f"picked{e}{a}", align_bytes=64)
                codes[e, a] = keep.tile([P, J], U32, name=f"codes{e}{a}", align_bytes=64)
                planes[e, a] = keep.tile([P, J], U8, name=f"plane{e}{a}", align_bytes=64)
        first_bank = psum.tile([P, J], F32, name="first_bank")
        later_bank = psum.tile([P, J], F32, name="later_bank")
        banks = {(e, i): later_bank if e + i else first_bank for e in range(2) for i in range(TILES)}
        sums = {(e, i): keep.tile([P, J], F32, name=f"sum{e}{i}") for e in range(2) for i in range(TILES)}
        both = [keep.tile([P, T], F32, name=f"both{i}") for i in range(TILES)]

        def cast(a, u, h, lo, hi, on_vector):
            tile, base = raw[a, u, h]
            dst = pairs[a, u][:, base + lo:base + hi].bitcast(BF16).rearrange("p (t e) -> p t e", e=2)
            src = tile[:, :, lo:hi].rearrange("p e t -> p t e")
            if on_vector:
                nc.vector.tensor_copy(dst, src)
            else:
                nc.scalar.activation(dst, src, ACT.Copy)

        def pick(e, a, u):
            nc.vector.tensor_copy(picked[e, a][:, u * J:(u + 1) * J], pairs[a, u][:].indirect(lists[e][:]))

        def weave(e, a, on_vector, tag):
            woven[e, a] = keep.tile([P, 2 * J], F32, name=f"woven{e}{a}", tag=tag, align_bytes=64)
            dst = woven[e, a][:].rearrange("p (j u) -> p j u", u=2)
            src = picked[e, a][:].rearrange("p (u j) -> p j u", u=2)
            if on_vector:
                nc.vector.tensor_copy(dst, src)
            else:
                nc.scalar.copy(dst, src)

        def quantize(e, a):
            nc.vector.quantize_mx(out=codes[e, a][:].bitcast(FP8X4), scales=planes[e, a][:], in_=woven[e, a][:].bitcast(BF16))

        def multiply(e, a, i):
            if e == 0:
                lhsT = wa[:, a, 2 * P * i:2 * P * (i + 1)].bitcast(FP4X4)
            else:
                lhsT = wb[:, a, 4 * P * i:4 * P * (i + 1)].bitcast(FP8X4)
            nc.tensor.matmul_mx(
                out=banks[e, i][:], lhsT=lhsT, lhsT_scale=w_scales[e][:, a, P * i:P * (i + 1)],
                rhs=codes[e, a][:].bitcast(FP8X4), rhs_scale=planes[e, a][:],
                start=(a == 0), stop=(a == PASSES - 1),
            )

        cast(0, 0, 0, 0, HALF, True)
        cast(0, 0, 1, 0, HALF, True)
        for a, u in ((0, 0), (0, 1), (1, 0), (1, 1)):
            if a + u:
                cast(a, u, 0, 0, HALF, False)
                if (a, u) == (0, 1):
                    cast(a, u, 1, 0, 256, False)
                    cast(a, u, 1, 256, HALF, True)
                else:
                    cast(a, u, 1, 0, HALF, False)
            pick(0, a, u)
            pick(1, a, u)
        weave(0, 0, False, "raw111")
        weave(1, 0, False, "picked00")
        weave(0, 1, False, "woven01")
        weave(1, 1, False, "woven11")
        for e in range(2):
            for a in range(PASSES):
                quantize(e, a)
        for a in range(PASSES):
            multiply(0, a, 0)
        nc.scalar.copy(sums[0, 0][:], banks[0, 0][:])

        for i in range(TILES):
            for e in range(2):
                if e + i:
                    for a in range(PASSES):
                        multiply(e, a, i)
                    nc.scalar.copy(sums[e, i][:], banks[e, i][:])
            sig = sigs[i]
            nc.scalar.activation(sig[:, :widths[i]], gates[i][:, :widths[i]], ACT.Sigmoid)
            page_p, page_q = pages[0, i % 2], pages[1, i % 2]
            nc.vector.tensor_copy(page_p[:].indirect(lists[1][:]), sums[0, i][:])
            nc.vector.tensor_copy(page_q[:].indirect(lists[0][:]), sums[1, i][:])
            rows = slice(i * P, (i + 1) * P)
            if i < TILES - 1:
                nc.gpsimd.tensor_tensor(both[i][:], page_p[:], page_q[:], ALU.add)
                nc.gpsimd.tensor_tensor(gates[i][:], both[i][:], sig[:], ALU.mult)
                nc.sync.dma_start(out[rows, :], gates[i][:])
            else:
                cuts = [slice(lo, hi) for lo, hi in zip(LAST_CUTS, LAST_CUTS[1:])]
                for cols in cuts:
                    nc.vector.tensor_tensor(both[i][:, cols], page_p[:, cols], page_q[:, cols], ALU.add)
                for cols in cuts:
                    nc.vector.tensor_tensor(gates[i][:, cols], both[i][:, cols], sig[:, cols], ALU.mult)
                    nc.sync.dma_start(out[rows, cols], gates[i][:, cols])
